import numpy as np
import ml_dtypes


def mxq(x, axis, fmt="e4m3"):
    dtype, down = {"e4m3": (ml_dtypes.float8_e4m3fn, 7), "e5m2": (ml_dtypes.float8_e5m2, 14)}[fmt]
    v = np.moveaxis(np.asarray(x, np.float32).astype(ml_dtypes.bfloat16).astype(np.float64), axis, -1)
    blocks = v.reshape(v.shape[:-1] + (-1, 32))
    amax = np.abs(blocks).max(-1, keepdims=True)
    byte = np.maximum(np.where(amax > 0, np.frexp(amax)[1] - 1 + 127, 0) - down, 1)
    scale = np.exp2(byte - 127.0)
    codes = (blocks / scale).astype(np.float32).astype(dtype).astype(np.float64)
    return np.moveaxis((codes * scale).reshape(v.shape), -1, axis)


WIDE = False


def mx_kscale(k):
    if not WIDE:
        return np.ones(k)
    levels = np.array([10, -10, 5, -5, 0])
    if k % 512:
        return np.exp2(np.random.permutation(np.resize(levels, k // 32))).repeat(32)
    a = np.empty((k // 512, 16))
    for p in range(k // 512):
        a[p, :8] = np.random.permutation(np.resize(levels, 8))
        for g in range(8):
            far = levels[np.abs(levels - a[p, g]) >= 10]
            a[p, g + 8] = far[np.random.randint(len(far))]
    return np.exp2(a.ravel()).repeat(32)


def f64(x):
    return np.asarray(x).astype(np.float64)


def striped(idx):
    return np.tile(idx.reshape(-1, 16).T, (8, 1)).astype(np.uint16)


def unstriped(offs):
    return offs[:16].T.reshape(-1).astype(np.int64)


E2M1 = np.array([0.0, 0.5, 1.0, 1.5, 2.0, 3.0, 4.0, 6.0, -0.0, -0.5, -1.0, -1.5, -2.0, -3.0, -4.0, -6.0])


def pack_weight(w, fmt):
    k, n = w.shape
    w = f64(np.asarray(w, np.float32).astype(ml_dtypes.bfloat16)).reshape(k // 32, 32, n)
    amax = np.abs(w).max(1)
    if fmt == "e4m3":
        byte = np.frexp(amax)[1] - 1 + 127 - 7
    else:
        mant, ex = np.frexp(amax / 6.0)
        byte = np.where(mant > 0.5, ex, ex - 1) + 127
    byte = np.clip(np.where(amax > 0, byte, 1), 1, 254)
    scaled = (w * np.exp2(127.0 - byte)[:, None, :]).reshape(k, n).astype(np.float32)
    by_word = np.ascontiguousarray(scaled.reshape(k // 512, 128, 4, n).transpose(0, 1, 3, 2))
    if fmt == "e4m3":
        words = by_word.astype(ml_dtypes.float8_e4m3fn).view(np.uint8)
    else:
        c = by_word.astype(ml_dtypes.float4_e2m1fn).view(np.uint8) & 0xF
        words = (c[..., 0::2] | (c[..., 1::2] << 4)).reshape(k // 512, 128, 2 * n)
    return np.ascontiguousarray(words), np.ascontiguousarray(byte.astype(np.uint8).reshape(k // 512, 16, n))


def unpack_weight(words, scales, fmt):
    g, _, n = scales.shape
    words = np.ascontiguousarray(words).reshape(g, 128, n, -1)
    if fmt == "e4m3":
        vals = words.view(ml_dtypes.float8_e4m3fn).astype(np.float64)
    else:
        nib = np.empty((g, 128, n, 4), np.uint8)
        nib[..., 0::2] = words & 0xF
        nib[..., 1::2] = words >> 4
        vals = E2M1[nib]
    vals = vals * np.repeat(np.exp2(scales.astype(np.float64) - 127.0), 8, axis=1)[..., None]
    return vals.transpose(0, 1, 3, 2).reshape(g * 512, n)


def relu(v):
    return np.maximum(v, 0.0)


K, T, E, C, H, N = 1024, 384, 12, 128, 512, 256
TOP = 4


def by_expert(wq, xq):
    return np.concatenate([wq[e].T @ xq[:, e * C:(e + 1) * C] for e in range(E)], axis=1)


def setup_inputs():
    n = np.random.standard_normal
    s = mx_kscale(K)[:, None]
    u = mx_kscale(H)
    deal = np.repeat(np.arange(E), C).reshape(TOP, T)[:, np.random.permutation(T)]
    deal = np.take_along_axis(deal, np.argsort(np.random.rand(TOP, T), axis=0), axis=0)
    for _ in range(8):
        s_, t_ = np.random.permutation(T).reshape(2, -1); r = np.random.randint(TOP, size=T // 2); x, y = deal[r, s_].copy(), deal[r, t_].copy()
        ok = ~((deal[:, s_] == y).any(0) | (deal[:, t_] == x).any(0)); deal[r[ok], s_[ok]] = y[ok]; deal[r[ok], t_[ok]] = x[ok]
    order = np.lexsort((np.random.rand(TOP * T), deal.reshape(-1)))
    slot_token = order % T; pos = np.empty(TOP * T, np.int64); pos[order] = np.arange(TOP * T); pos = pos.reshape(TOP, T)
    g = np.random.uniform(0.5, 1.5, (TOP, T)); g = g / g.sum(0)
    w1 = [pack_weight(m, "e2m1") for m in n((E, K, H)) / np.sqrt(K) / s[None] * u[None, None, :]]
    w2 = [pack_weight(m, "e2m1") for m in n((E, H, N)) / np.sqrt(H) / u[None, :, None]]
    return {
        "xT": (n((K, T)) * s).astype(np.float32),
        "w1_words": np.stack([m[0] for m in w1]),
        "w1_scales": np.stack([m[1] for m in w1]),
        "w2_words": np.stack([m[0] for m in w2]),
        "w2_scales": np.stack([m[1] for m in w2]),
        "gate": np.stack([np.tile(r, (N, 1)) for r in g]).astype(np.float32),
        "offs": striped(slot_token),
        "pos1": striped(pos[0]),
        "pos2": striped(pos[1]),
        "pos3": striped(pos[2]),
        "pos4": striped(pos[3]),
    }


def reference(xT, w1_words, w1_scales, w2_words, w2_scales, gate, offs, pos1, pos2, pos3, pos4):
    idx = unstriped(offs)
    w1 = np.stack([unpack_weight(w1_words[e], w1_scales[e], "e2m1") for e in range(E)])
    w2 = np.stack([unpack_weight(w2_words[e], w2_scales[e], "e2m1") for e in range(E)])
    xq = mxq(f64(xT)[:, idx], 0, "e4m3")
    h = relu(by_expert(w1, xq))
    y = by_expert(w2, mxq(h, 0, "e4m3"))
    return sum(f64(gate[r]) * y[:, unstriped(p)] for r, p in enumerate((pos1, pos2, pos3, pos4)))

@@ -1,0 +1,291 @@
+from contextlib import ExitStack
+
+import concourse.mybir as mybir
+from concourse.masks import make_identity
+
+F32 = mybir.dt.float32
+BF16 = mybir.dt.bfloat16
+I32 = mybir.dt.int32
+U32 = mybir.dt.uint32
+U16 = mybir.dt.uint16
+U8 = mybir.dt.uint8
+FP8X4 = mybir.dt.float8_e4m3fn_x4
+FP4X4 = mybir.dt.float4_e2m1fn_x4
+MULT = mybir.AluOpType.mult
+RELU = mybir.ActivationFunctionType.Relu
+
+K, T, E, C, H, N, TOP = 1024, 384, 12, 128, 512, 256, 4
+P = 128
+PASSES = K // 512
+WINDOW = 512
+SPLIT = 256
+FLOPS = 2 * TOP * T * (K * H + H * N)
+
+
+def tile_moe_tk_mlp_relu_kernel(
+    tc, xT, w1_words, w1_scales, w2_words, w2_scales, gate, offs, pos1, pos2, pos3, pos4, out
+):
+    nc = tc.nc
+    with ExitStack() as ctx:
+        keep = ctx.enter_context(tc.tile_pool(name="keep", bufs=1))
+        psum_a = ctx.enter_context(tc.psum_pool(name="psum_a", bufs=3))
+        psum_t = ctx.enter_context(tc.psum_pool(name="psum_t", bufs=2))
+        psum_y = ctx.enter_context(tc.psum_pool(name="psum_y", bufs=3))
+
+        w1_words32 = w1_words.bitcast(I32)
+        w1_scales32 = w1_scales.bitcast(I32)
+        w2_words32 = w2_words.bitcast(I32)
+        w2_scales32 = w2_scales.bitcast(I32)
+        raw = []
+        w1_at = {}
+        w1s_at = {}
+        w2_at = {}
+
+        def load_x(s):
+            r = keep.tile([P, 4, T], F32, name=f"raw{s}")
+            nc.sync.dma_start(out=r[:], in_=xT[512 * s : 512 * (s + 1), :].rearrange("(p j) w -> p j w", j=4))
+            raw.append(r)
+
+        def load_w1(queue, a, b):
+            w = keep.tile([P, b - a, PASSES, 2 * H], U8, name=f"w1w{a}", align_bytes=64)
+            queue.dma_start(
+                out=w[:].rearrange("p e s w -> p (e s) w").bitcast(I32),
+                in_=w1_words32[a:b].rearrange("e s p w -> p (e s) w"),
+            )
+            for e in range(a, b):
+                w1_at[e] = w[:, e - a]
+
+        def load_w1_scales(a, b, zero):
+            sc = keep.tile([P, b - a, PASSES, H], U8, name=f"w1s{a}", align_bytes=64)
+            zero.memset(sc[:].rearrange("p e s i -> p (e s i)").bitcast(I32), 0)
+            for q in range(4):
+                nc.sync.dma_start(
+                    out=sc[32 * q : 32 * q + 4].rearrange("p e s i -> p (e s) i").bitcast(I32),
+                    in_=w1_scales32[a:b, :, 4 * q : 4 * q + 4, :].rearrange("e s q i -> q (e s) i"),
+                )
+            for e in range(a, b):
+                w1s_at[e] = sc[:, e - a]
+
+        def load_w2(queue, a, b):
+            w = keep.tile([P, b - a, 2 * N], U8, name=f"w2w{a}", align_bytes=64)
+            queue.dma_start(out=w[:].bitcast(I32), in_=w2_words32[a:b, 0].rearrange("e p w -> p e w"))
+            for e in range(a, b):
+                w2_at[e] = w[:, e - a]
+
+        load_x(0)
+        x_bytes = keep.tile([P, WINDOW], U8, name="x_bytes", align_bytes=64)
+        nc.gpsimd.memset(x_bytes[:], 0)
+        late = keep.tile([P, TOP * T], U8, name="late", align_bytes=64)
+        nc.gpsimd.memset(late[:].bitcast(I32), 0)
+        load_x(1)
+        offs_t = keep.tile([P, TOP * T // 16], U16, name="offs_t")
+        nc.sync.dma_start(offs_t[:], offs)
+        load_w1_scales(0, 2, nc.vector)
+        load_w1(nc.sync, 0, 2)
+        load_w1(nc.sync, 2, 4)
+        w2s = keep.tile([P, E, N], U8, name="w2s", align_bytes=64)
+        nc.vector.memset(w2s[:].rearrange("p e n -> p (e n)").bitcast(I32), 0)
+        for q in range(4):
+            nc.sync.dma_start(
+                out=w2s[32 * q : 32 * q + 4].bitcast(I32),
+                in_=w2_scales32[:, 0, 4 * q : 4 * q + 4, :].rearrange("e q n -> q e n"),
+            )
+        load_w2(nc.sync, 0, 4)
+        load_w1_scales(2, E, nc.gpsimd)
+        load_w1(nc.sync, 4, 6)
+        load_w1(nc.sync, 6, 8)
+        load_w1(nc.sync, 8, 10)
+        load_w1(nc.sync, 10, 12)
+        load_w2(nc.sync, 4, 12)
+        pos_t = []
+        for r, pos in enumerate((pos1, pos2, pos3, pos4)):
+            pt = keep.tile([P, T // 16], U16, name=f"pos_t{r}")
+            nc.sync.dma_start(pt[:], pos)
+            pos_t.append(pt)
+        warm = keep.tile([P, 1], F32, name="warm")
+        nc.gpsimd.memset(warm[:], 0.0)
+        warm_out = keep.tile([P, 1], F32, name="warm_out")
+        nc.scalar.activation(warm_out[:], warm[:], RELU)
+        ident = keep.tile([P, P], F32, name="ident")
+        make_identity(nc, ident[:])
+        gate_t = []
+        for h in range(2):
+            g = keep.tile([P, TOP, T], F32, name=f"gate_t{h}")
+            nc.sync.dma_start(out=g[:], in_=gate[:, P * h : P * (h + 1), :].rearrange("r p t -> p r t"))
+            gate_t.append(g)
+
+        x_words = []
+        for s in range(PASSES):
+            w = keep.tile([P, WINDOW], I32, name=f"x_words{s}", align_bytes=64)
+            nc.vector.memset(w[:, T:], 0)
+            x_words.append(w)
+
+        def quantise_tokens(s):
+            xa = keep.tile([P, SPLIT, 4], BF16, name=f"xa{s}", align_bytes=64)
+            xb = keep.tile([P, T - SPLIT, 4], BF16, name=f"xb{s}", align_bytes=64)
+            nc.vector.tensor_copy(out=xa[:], in_=raw[s][:, :, :SPLIT].rearrange("p j w -> p w j"))
+            nc.scalar.copy(out=xb[:], in_=raw[s][:, :, SPLIT:].rearrange("p j w -> p w j"))
+            for x, cols in ((xa, slice(0, SPLIT)), (xb, slice(SPLIT, T))):
+                nc.vector.quantize_mx(
+                    out=x_words[s][:, cols].bitcast(FP8X4),
+                    scales=x_bytes[4 * s :, cols],
+                    in_=x[:].rearrange("p w j -> p (w j)"),
+                )
+
+        y_t = []
+        for h in range(2):
+            y = keep.tile([P, TOP * T], F32, name=f"y_t{h}")
+            y_t.append(y)
+
+        early_at = {}
+        words_at = {}
+        acc_at = {}
+        act_at = {}
+        turned_at = {}
+        ready_at = {}
+        hidden_at = {}
+        yp_at = {}
+
+        def gather_bytes(a, b, queue):
+            gb = keep.tile([P, C * (b - a)], U8, name=f"early{a}", align_bytes=64)
+            nc.vector.tensor_copy(gb[:], x_bytes[:].indirect(offs_t[:, C // 16 * a : C // 16 * b]))
+            for e in range(a, b):
+                early_at[e] = gb[:, C * (e - a) : C * (e - a + 1)]
+            if a == 0:
+                for q in range(4):
+                    queue.dma_start(
+                        out=late[32 * q : 32 * q + 4, C * a : C * b].bitcast(I32),
+                        in_=gb[32 * q + 4 : 32 * q + 8, :].bitcast(I32),
+                    )
+            else:
+                queue.dma_start(out=late[: P - 4, C * a : C * b].bitcast(I32), in_=gb[4:, :].bitcast(I32))
+
+        def gather_words(s, a, b):
+            gw = keep.tile([P, C * (b - a)], U32, name=f"words{s}_{a}", align_bytes=64)
+            nc.vector.tensor_copy(gw[:], x_words[s][:].bitcast(U32).indirect(offs_t[:, C // 16 * a : C // 16 * b]))
+            for e in range(a, b):
+                words_at[e, s] = gw[:, C * (e - a) : C * (e - a + 1)]
+
+        def first_product(e, s):
+            if s == 0:
+                acc_at[e] = psum_a.tile([P, H], F32, name="acc")
+            nc.tensor.matmul_mx(
+                out=acc_at[e][:],
+                lhsT=words_at[e, s].bitcast(FP8X4),
+                lhsT_scale=early_at[e] if s == 0 else late[:, C * e : C * (e + 1)],
+                rhs=w1_at[e][:, s, :].bitcast(FP4X4),
+                rhs_scale=w1s_at[e][:, s, :],
+                start=(s == 0),
+                stop=(s == PASSES - 1),
+            )
+
+        def relu(e):
+            act = keep.tile([P, H], BF16, name=f"act{e}")
+            nc.scalar.activation(
+                act[:].rearrange("p (u m d) -> p u m d", u=2, d=2),
+                acc_at[e][:].rearrange("p (m u d) -> p u m d", u=2, d=2),
+                RELU,
+            )
+            act_at[e] = act
+
+        def turn(e, a, b):
+            if e == a:
+                turned_at[a] = psum_t.tile([P, 2, 2, C], F32, name="tp")
+            for u in range(2):
+                nc.tensor.transpose(
+                    turned_at[a][:, e - a, u, :], act_at[e][:].bitcast(F32)[:, C * u : C * (u + 1)], ident[:]
+                )
+
+        def interleave(copy, a, b):
+            ht = keep.tile([P, (b - a) * C * 4], BF16, name=f"ht{a}", align_bytes=64)
+            copy(
+                out=ht[:].bitcast(F32).rearrange("p (i r u) -> p i r u", i=b - a, u=2),
+                in_=turned_at[a][:, : b - a].rearrange("p i u r -> p i r u"),
+            )
+            ready_at[a] = ht
+
+        def quantise_hidden(a, b):
+            hw = keep.tile([P, (b - a) * C], U32, name=f"hw{a}", align_bytes=64)
+            hb = keep.tile([P, (b - a) * C], U8, name=f"hb{a}", align_bytes=64)
+            nc.vector.quantize_mx(out=hw[:].bitcast(FP8X4), scales=hb[:], in_=ready_at[a][:])
+            for e in range(a, b):
+                cols = slice(C * (e - a), C * (e - a + 1))
+                hidden_at[e] = (hw[:, cols], hb[:, cols])
+
+        def second_product(e):
+            if e % 2 == 0:
+                yp_at[e // 2] = psum_y.tile([P, 2, 2 * C], F32, name="yp")
+            hw, hb = hidden_at[e]
+            for h in range(2):
+                nc.tensor.matmul_mx(
+                    out=yp_at[e // 2][:, h, C * (e % 2) : C * (e % 2 + 1)],
+                    lhsT=w2_at[e][:, 2 * P * h : 2 * P * (h + 1)].bitcast(FP4X4),
+                    lhsT_scale=w2s[:, e, P * h : P * (h + 1)],
+                    rhs=hw.bitcast(FP8X4),
+                    rhs_scale=hb,
+                    start=True,
+                    stop=True,
+                )
+
+        def keep_y(copy, e, h):
+            copy(out=y_t[h][:, C * e : C * (e + 2)], in_=yp_at[e // 2][:, h, :])
+
+        on_scalar = nc.scalar.copy
+        on_vector = nc.vector.tensor_copy
+        quantise_tokens(0)
+        gather_words(0, 0, 2)
+        quantise_tokens(1)
+        gather_bytes(0, 3, nc.scalar)
+        gather_words(1, 0, 2)
+        plan = []
+        for e, q in ((3, nc.gpsimd), (6, nc.gpsimd), (9, nc.gpsimd)):
+            plan.append((e - 5, gather_bytes, (e, e + 3, q)))
+        for e in range(2, E, 2):
+            for s in range(PASSES):
+                plan.append((e - 3 + 0.01 * s, gather_words, (s, e, e + 2)))
+        for e in range(E):
+            plan.append((e - 0.5, first_product, (e, 0)))
+            plan.append((e + 0.1, first_product, (e, 1)))
+            plan.append((e + 0.2, relu, (e,)))
+        for a, b in ((0, 2), (2, 4), (4, 6), (6, 8), (8, 10), (10, 11), (11, 12)):
+            for e in range(a, b):
+                plan.append((e + 1.5 + 0.3, turn, (e, a, b)))
+                plan.append((b - 1 + 2.5 + 3 + 0.6, second_product, (e,)))
+            plan.append((b - 1 + 1.5 + 0.4, interleave, (on_scalar if a < 4 else on_vector, a, b)))
+            plan.append((b - 1 + 2.5 + 0.5, quantise_hidden, (a, b)))
+        for e in range(0, E, 2):
+            for h in range(2):
+                plan.append((e + 1 + 2.5 + 3.5 + 0.7, keep_y, (on_vector if h == 1 and e >= 8 else on_scalar, e, h)))
+        for when, step, what in sorted(plan, key=lambda entry: entry[0]):
+            step(*what)
+
+        z = []
+        part = []
+        o = []
+        for h in range(2):
+            zt = keep.tile([P, TOP, T], F32, name=f"z{h}")
+            pt = keep.tile([P, 2, T], F32, name=f"part{h}")
+            ot = keep.tile([P, T], F32, name=f"o{h}")
+            z.append(zt)
+            part.append(pt)
+            o.append(ot)
+
+        def fetch(h, r):
+            nc.vector.tensor_tensor(z[h][:, r, :], y_t[h][:].indirect(pos_t[r][:]), gate_t[h][:, r, :], MULT)
+
+        def store(h):
+            nc.sync.dma_start(out=out[P * h : P * (h + 1), :], in_=o[h][:])
+
+        for r in range(TOP):
+            fetch(0, r)
+        fetch(1, 0)
+        nc.vector.tensor_add(part[0][:], z[0][:, 0:2, :], z[0][:, 2:4, :])
+        fetch(1, 1)
+        nc.vector.tensor_add(o[0][:], part[0][:, 0, :], part[0][:, 1, :])
+        store(0)
+        fetch(1, 2)
+        nc.vector.tensor_add(part[1][:, 0, :], z[1][:, 0, :], z[1][:, 1, :])
+        fetch(1, 3)
+        nc.vector.tensor_add(part[1][:, 1, :], part[1][:, 0, :], z[1][:, 2, :])
+        nc.vector.tensor_add(o[1][:], part[1][:, 1, :], z[1][:, 3, :])
+        store(1)

@@ -18,7 +18,7 @@ K, T, E, C, H, N, TOP = 1024, 384, 12, 128, 512, 256, 4
 P = 128
 PASSES = K // 512
 WINDOW = 512
-SPLIT = 256
+SPLIT = (256, 128)
 FLOPS = 2 * TOP * T * (K * H + H * N)
 
 
@@ -28,9 +28,14 @@ def tile_moe_tk_mlp_relu_kernel(
     nc = tc.nc
     with ExitStack() as ctx:
         keep = ctx.enter_context(tc.tile_pool(name="keep", bufs=1))
-        psum_a = ctx.enter_context(tc.psum_pool(name="psum_a", bufs=3))
+        w1_pool = ctx.enter_context(tc.tile_pool(name="w1_pool", bufs=4))
+        hand = ctx.enter_context(tc.tile_pool(name="hand", bufs=1))
+        words_pool = []
+        for s in range(PASSES):
+            words_pool.append(ctx.enter_context(tc.tile_pool(name=f"words_pool{s}", bufs=(2, 2)[s])))
+        psum_a = ctx.enter_context(tc.psum_pool(name="psum_a", bufs=4))
         psum_t = ctx.enter_context(tc.psum_pool(name="psum_t", bufs=2))
-        psum_y = ctx.enter_context(tc.psum_pool(name="psum_y", bufs=3))
+        psum_y = ctx.enter_context(tc.psum_pool(name="psum_y", bufs=2))
 
         w1_words32 = w1_words.bitcast(I32)
         w1_scales32 = w1_scales.bitcast(I32)
@@ -46,73 +51,72 @@ def tile_moe_tk_mlp_relu_kernel(
             nc.sync.dma_start(out=r[:], in_=xT[512 * s : 512 * (s + 1), :].rearrange("(p j) w -> p j w", j=4))
             raw.append(r)
 
-        def load_w1(queue, a, b):
-            w = keep.tile([P, b - a, PASSES, 2 * H], U8, name=f"w1w{a}", align_bytes=64)
-            queue.dma_start(
+        def load_w1(a):
+            w = w1_pool.tile([P, 2, PASSES, 2 * H], U8, name="w1w", align_bytes=64)
+            nc.sync.dma_start(
                 out=w[:].rearrange("p e s w -> p (e s) w").bitcast(I32),
-                in_=w1_words32[a:b].rearrange("e s p w -> p (e s) w"),
+                in_=w1_words32[a : a + 2].rearrange("e s p w -> p (e s) w"),
             )
-            for e in range(a, b):
-                w1_at[e] = w[:, e - a]
+            for e in range(2):
+                w1_at[a + e] = w[:, e]
 
-        def load_w1_scales(a, b, zero):
+        def load_w1_scales(queue, zero, a, b):
             sc = keep.tile([P, b - a, PASSES, H], U8, name=f"w1s{a}", align_bytes=64)
             zero.memset(sc[:].rearrange("p e s i -> p (e s i)").bitcast(I32), 0)
             for q in range(4):
-                nc.sync.dma_start(
+                queue.dma_start(
                     out=sc[32 * q : 32 * q + 4].rearrange("p e s i -> p (e s) i").bitcast(I32),
                     in_=w1_scales32[a:b, :, 4 * q : 4 * q + 4, :].rearrange("e s q i -> q (e s) i"),
                 )
             for e in range(a, b):
                 w1s_at[e] = sc[:, e - a]
 
-        def load_w2(queue, a, b):
-            w = keep.tile([P, b - a, 2 * N], U8, name=f"w2w{a}", align_bytes=64)
-            queue.dma_start(out=w[:].bitcast(I32), in_=w2_words32[a:b, 0].rearrange("e p w -> p e w"))
+        def load_w2(a, b):
+            w = hand.tile([P, b - a, 2 * N], U8, name="hand", align_bytes=64)
+            nc.sync.dma_start(out=w[:].bitcast(I32), in_=w2_words32[a:b, 0].rearrange("e p w -> p e w"))
             for e in range(a, b):
                 w2_at[e] = w[:, e - a]
 
-        load_x(0)
-        x_bytes = keep.tile([P, WINDOW], U8, name="x_bytes", align_bytes=64)
-        nc.gpsimd.memset(x_bytes[:], 0)
-        late = keep.tile([P, TOP * T], U8, name="late", align_bytes=64)
-        nc.gpsimd.memset(late[:].bitcast(I32), 0)
-        load_x(1)
-        offs_t = keep.tile([P, TOP * T // 16], U16, name="offs_t")
-        nc.sync.dma_start(offs_t[:], offs)
-        load_w1_scales(0, 2, nc.vector)
-        load_w1(nc.sync, 0, 2)
-        load_w1(nc.sync, 2, 4)
-        w2s = keep.tile([P, E, N], U8, name="w2s", align_bytes=64)
-        nc.vector.memset(w2s[:].rearrange("p e n -> p (e n)").bitcast(I32), 0)
-        for q in range(4):
-            nc.sync.dma_start(
-                out=w2s[32 * q : 32 * q + 4].bitcast(I32),
-                in_=w2_scales32[:, 0, 4 * q : 4 * q + 4, :].rearrange("e q n -> q e n"),
-            )
-        load_w2(nc.sync, 0, 4)
-        load_w1_scales(2, E, nc.gpsimd)
-        load_w1(nc.sync, 4, 6)
-        load_w1(nc.sync, 6, 8)
-        load_w1(nc.sync, 8, 10)
-        load_w1(nc.sync, 10, 12)
-        load_w2(nc.sync, 4, 12)
-        pos_t = []
-        for r, pos in enumerate((pos1, pos2, pos3, pos4)):
-            pt = keep.tile([P, T // 16], U16, name=f"pos_t{r}")
-            nc.sync.dma_start(pt[:], pos)
-            pos_t.append(pt)
         warm = keep.tile([P, 1], F32, name="warm")
         nc.gpsimd.memset(warm[:], 0.0)
         warm_out = keep.tile([P, 1], F32, name="warm_out")
         nc.scalar.activation(warm_out[:], warm[:], RELU)
         ident = keep.tile([P, P], F32, name="ident")
         make_identity(nc, ident[:])
-        gate_t = []
-        for h in range(2):
-            g = keep.tile([P, TOP, T], F32, name=f"gate_t{h}")
-            nc.sync.dma_start(out=g[:], in_=gate[:, P * h : P * (h + 1), :].rearrange("r p t -> p r t"))
-            gate_t.append(g)
+        load_x(0)
+        load_x(1)
+        offs_t = keep.tile([P, TOP * T // 16], U16, name="offs_t")
+        nc.sync.dma_start(offs_t[:], offs)
+        load_w1(0)
+        load_w1_scales(nc.sync, nc.vector, 0, 4)
+        load_w1(2)
+        load_w1(4)
+        late = keep.tile([P, TOP * T], U8, name="late", align_bytes=64)
+        nc.gpsimd.memset(late[:].bitcast(I32), 0)
+        w2s = keep.tile([P, E, N], U8, name="w2s", align_bytes=64)
+        nc.gpsimd.memset(w2s[:].rearrange("p e n -> p (e n)").bitcast(I32), 0)
+        load_w1_scales(nc.gpsimd, nc.gpsimd, 4, E)
+        x_bytes = keep.tile([P, WINDOW], U8, name="x_bytes", align_bytes=64)
+        nc.vector.memset(x_bytes[:].bitcast(I32), 0)
+        pos_t = []
+        gate_t = {}
+
+        def load_w2_scales():
+            for q in range(4):
+                nc.scalar.dma_start(
+                    out=w2s[32 * q : 32 * q + 4].bitcast(I32),
+                    in_=w2_scales32[:, 0, 4 * q : 4 * q + 4, :].rearrange("e q n -> q e n"),
+                )
+
+        def load_lists():
+            for r, pos in enumerate((pos1, pos2, pos3, pos4)):
+                pt = keep.tile([P, T // 16], U16, name=f"pos_t{r}")
+                nc.sync.dma_start(pt[:], pos)
+                pos_t.append(pt)
+
+        def load_gate(h):
+            gate_t[h] = w1_pool.tile([P, TOP, T], F32, name="w1w", align_bytes=64)
+            nc.sync.dma_start(out=gate_t[h][:], in_=gate[:, P * h : P * (h + 1), :].rearrange("r p t -> p r t"))
 
         x_words = []
         for s in range(PASSES):
@@ -121,11 +125,12 @@ def tile_moe_tk_mlp_relu_kernel(
             x_words.append(w)
 
         def quantise_tokens(s):
-            xa = keep.tile([P, SPLIT, 4], BF16, name=f"xa{s}", align_bytes=64)
-            xb = keep.tile([P, T - SPLIT, 4], BF16, name=f"xb{s}", align_bytes=64)
-            nc.vector.tensor_copy(out=xa[:], in_=raw[s][:, :, :SPLIT].rearrange("p j w -> p w j"))
-            nc.scalar.copy(out=xb[:], in_=raw[s][:, :, SPLIT:].rearrange("p j w -> p w j"))
-            for x, cols in ((xa, slice(0, SPLIT)), (xb, slice(SPLIT, T))):
+            cut = SPLIT[s]
+            xa = keep.tile([P, cut, 4], BF16, name=f"xa{s}", align_bytes=64)
+            xb = keep.tile([P, T - cut, 4], BF16, name=f"xb{s}", align_bytes=64)
+            nc.vector.tensor_copy(out=xa[:], in_=raw[s][:, :, :cut].rearrange("p j w -> p w j"))
+            nc.scalar.copy(out=xb[:], in_=raw[s][:, :, cut:].rearrange("p j w -> p w j"))
+            for x, cols in ((xa, slice(0, cut)), (xb, slice(cut, T))):
                 nc.vector.quantize_mx(
                     out=x_words[s][:, cols].bitcast(FP8X4),
                     scales=x_bytes[4 * s :, cols],
@@ -146,22 +151,17 @@ def tile_moe_tk_mlp_relu_kernel(
         hidden_at = {}
         yp_at = {}
 
-        def gather_bytes(a, b, queue):
-            gb = keep.tile([P, C * (b - a)], U8, name=f"early{a}", align_bytes=64)
+        def gather_bytes(a, b):
+            pool = hand if a == 0 else keep
+            gb = pool.tile([P, C * (b - a)], U8, name="hand" if a == 0 else f"early{a}", align_bytes=64)
             nc.vector.tensor_copy(gb[:], x_bytes[:].indirect(offs_t[:, C // 16 * a : C // 16 * b]))
             for e in range(a, b):
                 early_at[e] = gb[:, C * (e - a) : C * (e - a + 1)]
-            if a == 0:
-                for q in range(4):
-                    queue.dma_start(
-                        out=late[32 * q : 32 * q + 4, C * a : C * b].bitcast(I32),
-                        in_=gb[32 * q + 4 : 32 * q + 8, :].bitcast(I32),
-                    )
-            else:
-                queue.dma_start(out=late[: P - 4, C * a : C * b].bitcast(I32), in_=gb[4:, :].bitcast(I32))
+            queue = nc.sync
+            queue.dma_start(out=late[:112, C * a : C * b].bitcast(I32), in_=gb[4:116, :].bitcast(I32))
 
         def gather_words(s, a, b):
-            gw = keep.tile([P, C * (b - a)], U32, name=f"words{s}_{a}", align_bytes=64)
+            gw = words_pool[s].tile([P, C * (b - a)], U32, name=f"words{s}", align_bytes=64)
             nc.vector.tensor_copy(gw[:], x_words[s][:].bitcast(U32).indirect(offs_t[:, C // 16 * a : C // 16 * b]))
             for e in range(a, b):
                 words_at[e, s] = gw[:, C * (e - a) : C * (e - a + 1)]
@@ -235,27 +235,36 @@ def tile_moe_tk_mlp_relu_kernel(
         quantise_tokens(0)
         gather_words(0, 0, 2)
         quantise_tokens(1)
-        gather_bytes(0, 3, nc.scalar)
+        gather_bytes(0, 2)
         gather_words(1, 0, 2)
-        plan = []
-        for e, q in ((3, nc.gpsimd), (6, nc.gpsimd), (9, nc.gpsimd)):
-            plan.append((e - 5, gather_bytes, (e, e + 3, q)))
+        load_w2_scales()
+        load_w2(0, E)
+        plan = [
+            (-3.45, load_w1, (6,)),
+            (1.15, load_w1, (8,)),
+            (3.15, load_w1, (10,)),
+            (5.15, load_gate, (0,)),
+            (7.15, load_gate, (1,)),
+            (7.2, load_lists, ()),
+        ]
+        for a, b in ((2, 4), (4, 6), (6, 9), (9, 12)):
+            plan.append((a - 5.5, gather_bytes, (a, b)))
         for e in range(2, E, 2):
             for s in range(PASSES):
-                plan.append((e - 3 + 0.01 * s, gather_words, (s, e, e + 2)))
+                plan.append((e - 2.5 + 0.03 * s, gather_words, (s, e, e + 2)))
         for e in range(E):
-            plan.append((e - 0.5, first_product, (e, 0)))
+            plan.append((e - 1.5, first_product, (e, 0)))
             plan.append((e + 0.1, first_product, (e, 1)))
             plan.append((e + 0.2, relu, (e,)))
         for a, b in ((0, 2), (2, 4), (4, 6), (6, 8), (8, 10), (10, 11), (11, 12)):
             for e in range(a, b):
-                plan.append((e + 1.5 + 0.3, turn, (e, a, b)))
-                plan.append((b - 1 + 2.5 + 3 + 0.6, second_product, (e,)))
-            plan.append((b - 1 + 1.5 + 0.4, interleave, (on_scalar if a < 4 else on_vector, a, b)))
-            plan.append((b - 1 + 2.5 + 0.5, quantise_hidden, (a, b)))
+                plan.append((b - 1 + 2 + 0.3, turn, (e, a, b)))
+                plan.append((b - 1 + 3 + 1.5 + 0.6, second_product, (e,)))
+            plan.append((b - 1 + 2.5 + 0.4, interleave, (on_vector if 6 <= a < 10 else on_scalar, a, b)))
+            plan.append((b - 1 + 3 + 0.5, quantise_hidden, (a, b)))
         for e in range(0, E, 2):
             for h in range(2):
-                plan.append((e + 1 + 2.5 + 3.5 + 0.7, keep_y, (on_vector if h == 1 and e >= 8 else on_scalar, e, h)))
+                plan.append((e + 1 + 3 + 2 + 0.7, keep_y, (on_vector if h == 1 and e >= 0 else on_scalar, e, h)))
         for when, step, what in sorted(plan, key=lambda entry: entry[0]):
             step(*what)
 

@@ -29,10 +29,12 @@ def tile_moe_tk_mlp_relu_kernel(
     with ExitStack() as ctx:
         keep = ctx.enter_context(tc.tile_pool(name="keep", bufs=1))
         w1_pool = ctx.enter_context(tc.tile_pool(name="w1_pool", bufs=4))
-        hand = ctx.enter_context(tc.tile_pool(name="hand", bufs=1))
         words_pool = []
         for s in range(PASSES):
             words_pool.append(ctx.enter_context(tc.tile_pool(name=f"words_pool{s}", bufs=(2, 2)[s])))
+        bytes_pool = []
+        for s in range(PASSES):
+            bytes_pool.append(ctx.enter_context(tc.tile_pool(name=f"bytes_pool{s}", bufs=2)))
         psum_a = ctx.enter_context(tc.psum_pool(name="psum_a", bufs=4))
         psum_t = ctx.enter_context(tc.psum_pool(name="psum_t", bufs=2))
         psum_y = ctx.enter_context(tc.psum_pool(name="psum_y", bufs=2))
@@ -60,9 +62,12 @@ def tile_moe_tk_mlp_relu_kernel(
             for e in range(2):
                 w1_at[a + e] = w[:, e]
 
-        def load_w1_scales(queue, zero, a, b):
+        def zero_w1_scales(engine, a, b):
             sc = keep.tile([P, b - a, PASSES, H], U8, name=f"w1s{a}", align_bytes=64)
-            zero.memset(sc[:].rearrange("p e s i -> p (e s i)").bitcast(I32), 0)
+            engine.memset(sc[:].rearrange("p e s i -> p (e s i)").bitcast(I32), 0)
+            return sc
+
+        def load_w1_scales(queue, sc, a, b):
             for q in range(4):
                 queue.dma_start(
                     out=sc[32 * q : 32 * q + 4].rearrange("p e s i -> p (e s) i").bitcast(I32),
@@ -72,7 +77,7 @@ def tile_moe_tk_mlp_relu_kernel(
                 w1s_at[e] = sc[:, e - a]
 
         def load_w2(a, b):
-            w = hand.tile([P, b - a, 2 * N], U8, name="hand", align_bytes=64)
+            w = keep.tile([P, b - a, 2 * N], U8, name="w2w", align_bytes=64)
             nc.sync.dma_start(out=w[:].bitcast(I32), in_=w2_words32[a:b, 0].rearrange("e p w -> p e w"))
             for e in range(a, b):
                 w2_at[e] = w[:, e - a]
@@ -88,22 +93,24 @@ def tile_moe_tk_mlp_relu_kernel(
         offs_t = keep.tile([P, TOP * T // 16], U16, name="offs_t")
         nc.sync.dma_start(offs_t[:], offs)
         load_w1(0)
-        load_w1_scales(nc.sync, nc.vector, 0, 4)
+        first_scales = zero_w1_scales(nc.vector, 0, 4)
+        load_w1_scales(nc.sync, first_scales, 0, 4)
         load_w1(2)
         load_w1(4)
-        late = keep.tile([P, TOP * T], U8, name="late", align_bytes=64)
-        nc.gpsimd.memset(late[:].bitcast(I32), 0)
         w2s = keep.tile([P, E, N], U8, name="w2s", align_bytes=64)
         nc.gpsimd.memset(w2s[:].rearrange("p e n -> p (e n)").bitcast(I32), 0)
-        load_w1_scales(nc.gpsimd, nc.gpsimd, 4, E)
-        x_bytes = keep.tile([P, WINDOW], U8, name="x_bytes", align_bytes=64)
-        nc.vector.memset(x_bytes[:].bitcast(I32), 0)
+        other_scales = zero_w1_scales(nc.gpsimd, 4, E)
+        x_bytes = []
+        for s in range(PASSES):
+            b = keep.tile([P, WINDOW], U8, name=f"x_bytes{s}", align_bytes=64)
+            nc.vector.memset(b[:].bitcast(I32), 0)
+            x_bytes.append(b)
         pos_t = []
         gate_t = {}
 
         def load_w2_scales():
             for q in range(4):
-                nc.scalar.dma_start(
+                nc.sync.dma_start(
                     out=w2s[32 * q : 32 * q + 4].bitcast(I32),
                     in_=w2_scales32[:, 0, 4 * q : 4 * q + 4, :].rearrange("e q n -> q e n"),
                 )
@@ -133,7 +140,7 @@ def tile_moe_tk_mlp_relu_kernel(
             for x, cols in ((xa, slice(0, cut)), (xb, slice(cut, T))):
                 nc.vector.quantize_mx(
                     out=x_words[s][:, cols].bitcast(FP8X4),
-                    scales=x_bytes[4 * s :, cols],
+                    scales=x_bytes[s][:, cols],
                     in_=x[:].rearrange("p w j -> p (w j)"),
                 )
 
@@ -142,7 +149,7 @@ def tile_moe_tk_mlp_relu_kernel(
             y = keep.tile([P, TOP * T], F32, name=f"y_t{h}")
             y_t.append(y)
 
-        early_at = {}
+        bytes_at = {}
         words_at = {}
         acc_at = {}
         act_at = {}
@@ -151,14 +158,11 @@ def tile_moe_tk_mlp_relu_kernel(
         hidden_at = {}
         yp_at = {}
 
-        def gather_bytes(a, b):
-            pool = hand if a == 0 else keep
-            gb = pool.tile([P, C * (b - a)], U8, name="hand" if a == 0 else f"early{a}", align_bytes=64)
-            nc.vector.tensor_copy(gb[:], x_bytes[:].indirect(offs_t[:, C // 16 * a : C // 16 * b]))
+        def gather_bytes(s, a, b):
+            gb = bytes_pool[s].tile([P, C * (b - a)], U8, name=f"bytes{s}", align_bytes=64)
+            nc.vector.tensor_copy(gb[:], x_bytes[s][:].indirect(offs_t[:, C // 16 * a : C // 16 * b]))
             for e in range(a, b):
-                early_at[e] = gb[:, C * (e - a) : C * (e - a + 1)]
-            queue = nc.sync
-            queue.dma_start(out=late[:112, C * a : C * b].bitcast(I32), in_=gb[4:116, :].bitcast(I32))
+                bytes_at[e, s] = gb[:, C * (e - a) : C * (e - a + 1)]
 
         def gather_words(s, a, b):
             gw = words_pool[s].tile([P, C * (b - a)], U32, name=f"words{s}", align_bytes=64)
@@ -172,7 +176,7 @@ def tile_moe_tk_mlp_relu_kernel(
             nc.tensor.matmul_mx(
                 out=acc_at[e][:],
                 lhsT=words_at[e, s].bitcast(FP8X4),
-                lhsT_scale=early_at[e] if s == 0 else late[:, C * e : C * (e + 1)],
+                lhsT_scale=bytes_at[e, s],
                 rhs=w1_at[e][:, s, :].bitcast(FP4X4),
                 rhs_scale=w1s_at[e][:, s, :],
                 start=(s == 0),
@@ -233,13 +237,15 @@ def tile_moe_tk_mlp_relu_kernel(
         on_scalar = nc.scalar.copy
         on_vector = nc.vector.tensor_copy
         quantise_tokens(0)
+        gather_bytes(0, 0, 2)
         gather_words(0, 0, 2)
         quantise_tokens(1)
-        gather_bytes(0, 2)
+        gather_bytes(1, 0, 2)
         gather_words(1, 0, 2)
-        load_w2_scales()
+        load_w1_scales(nc.scalar, other_scales, 4, E)
         load_w2(0, E)
         plan = [
+            (-1.4, load_w2_scales, ()),
             (-3.45, load_w1, (6,)),
             (1.15, load_w1, (8,)),
             (3.15, load_w1, (10,)),
@@ -247,11 +253,10 @@ def tile_moe_tk_mlp_relu_kernel(
             (7.15, load_gate, (1,)),
             (7.2, load_lists, ()),
         ]
-        for a, b in ((2, 4), (4, 6), (6, 9), (9, 12)):
-            plan.append((a - 5.5, gather_bytes, (a, b)))
         for e in range(2, E, 2):
             for s in range(PASSES):
-                plan.append((e - 2.5 + 0.03 * s, gather_words, (s, e, e + 2)))
+                plan.append((e - 2 + 0.03 * s, gather_bytes, (s, e, e + 2)))
+                plan.append((e - 2 + 0.03 * s + 0.01, gather_words, (s, e, e + 2)))
         for e in range(E):
             plan.append((e - 1.5, first_product, (e, 0)))
             plan.append((e + 0.1, first_product, (e, 1)))
@@ -260,11 +265,11 @@ def tile_moe_tk_mlp_relu_kernel(
             for e in range(a, b):
                 plan.append((b - 1 + 2 + 0.3, turn, (e, a, b)))
                 plan.append((b - 1 + 3 + 1.5 + 0.6, second_product, (e,)))
-            plan.append((b - 1 + 2.5 + 0.4, interleave, (on_vector if 6 <= a < 10 else on_scalar, a, b)))
+            plan.append((b - 1 + 2.5 + 0.4, interleave, (on_vector if 99 <= a < 99 else on_scalar, a, b)))
             plan.append((b - 1 + 3 + 0.5, quantise_hidden, (a, b)))
         for e in range(0, E, 2):
             for h in range(2):
-                plan.append((e + 1 + 3 + 2 + 0.7, keep_y, (on_vector if h == 1 and e >= 0 else on_scalar, e, h)))
+                plan.append((e + 1 + 3 + 2 + 0.7, keep_y, (on_vector if h == 1 and e >= 99 else on_scalar, e, h)))
         for when, step, what in sorted(plan, key=lambda entry: entry[0]):
             step(*what)
 
@@ -288,13 +293,13 @@ def tile_moe_tk_mlp_relu_kernel(
         for r in range(TOP):
             fetch(0, r)
         fetch(1, 0)
-        nc.vector.tensor_add(part[0][:], z[0][:, 0:2, :], z[0][:, 2:4, :])
         fetch(1, 1)
-        nc.vector.tensor_add(o[0][:], part[0][:, 0, :], part[0][:, 1, :])
-        store(0)
+        nc.vector.tensor_add(part[0][:], z[0][:, 0:2, :], z[0][:, 2:4, :])
         fetch(1, 2)
         nc.vector.tensor_add(part[1][:, 0, :], z[1][:, 0, :], z[1][:, 1, :])
-        fetch(1, 3)
+        nc.vector.tensor_add(o[0][:], part[0][:, 0, :], part[0][:, 1, :])
+        store(0)
         nc.vector.tensor_add(part[1][:, 1, :], part[1][:, 0, :], z[1][:, 2, :])
+        fetch(1, 3)
         nc.vector.tensor_add(o[1][:], part[1][:, 1, :], z[1][:, 3, :])
         store(1)

@@ -18,7 +18,6 @@ K, T, E, C, H, N, TOP = 1024, 384, 12, 128, 512, 256, 4
 P = 128
 PASSES = K // 512
 WINDOW = 512
-SPLIT = (256, 128)
 FLOPS = 2 * TOP * T * (K * H + H * N)
 
 
@@ -28,7 +27,6 @@ def tile_moe_tk_mlp_relu_kernel(
     nc = tc.nc
     with ExitStack() as ctx:
         keep = ctx.enter_context(tc.tile_pool(name="keep", bufs=1))
-        w1_pool = ctx.enter_context(tc.tile_pool(name="w1_pool", bufs=4))
         words_pool = []
         for s in range(PASSES):
             words_pool.append(ctx.enter_context(tc.tile_pool(name=f"words_pool{s}", bufs=(2, 2)[s])))
@@ -54,7 +52,7 @@ def tile_moe_tk_mlp_relu_kernel(
             raw.append(r)
 
         def load_w1(a):
-            w = w1_pool.tile([P, 2, PASSES, 2 * H], U8, name="w1w", align_bytes=64)
+            w = keep.tile([P, 2, PASSES, 2 * H], U8, name=f"w1w{a}", align_bytes=64)
             nc.sync.dma_start(
                 out=w[:].rearrange("p e s w -> p (e s) w").bitcast(I32),
                 in_=w1_words32[a : a + 2].rearrange("e s p w -> p (e s) w"),
@@ -62,14 +60,11 @@ def tile_moe_tk_mlp_relu_kernel(
             for e in range(2):
                 w1_at[a + e] = w[:, e]
 
-        def zero_w1_scales(engine, a, b):
+        def load_w1_scales(a, b, zero):
             sc = keep.tile([P, b - a, PASSES, H], U8, name=f"w1s{a}", align_bytes=64)
-            engine.memset(sc[:].rearrange("p e s i -> p (e s i)").bitcast(I32), 0)
-            return sc
-
-        def load_w1_scales(queue, sc, a, b):
+            zero.memset(sc[:].rearrange("p e s i -> p (e s i)").bitcast(I32), 0)
             for q in range(4):
-                queue.dma_start(
+                nc.sync.dma_start(
                     out=sc[32 * q : 32 * q + 4].rearrange("p e s i -> p (e s) i").bitcast(I32),
                     in_=w1_scales32[a:b, :, 4 * q : 4 * q + 4, :].rearrange("e s q i -> q (e s) i"),
                 )
@@ -77,7 +72,7 @@ def tile_moe_tk_mlp_relu_kernel(
                 w1s_at[e] = sc[:, e - a]
 
         def load_w2(a, b):
-            w = keep.tile([P, b - a, 2 * N], U8, name="w2w", align_bytes=64)
+            w = keep.tile([P, b - a, 2 * N], U8, name=f"w2w{a}", align_bytes=64)
             nc.sync.dma_start(out=w[:].bitcast(I32), in_=w2_words32[a:b, 0].rearrange("e p w -> p e w"))
             for e in range(a, b):
                 w2_at[e] = w[:, e - a]
@@ -93,37 +88,37 @@ def tile_moe_tk_mlp_relu_kernel(
         offs_t = keep.tile([P, TOP * T // 16], U16, name="offs_t")
         nc.sync.dma_start(offs_t[:], offs)
         load_w1(0)
-        first_scales = zero_w1_scales(nc.vector, 0, 4)
-        load_w1_scales(nc.sync, first_scales, 0, 4)
+        load_w1_scales(0, 4, nc.vector)
         load_w1(2)
         load_w1(4)
+        load_w1_scales(4, E, nc.gpsimd)
         w2s = keep.tile([P, E, N], U8, name="w2s", align_bytes=64)
         nc.gpsimd.memset(w2s[:].rearrange("p e n -> p (e n)").bitcast(I32), 0)
-        other_scales = zero_w1_scales(nc.gpsimd, 4, E)
+        for q in range(4):
+            nc.sync.dma_start(
+                out=w2s[32 * q : 32 * q + 4].bitcast(I32),
+                in_=w2_scales32[:, 0, 4 * q : 4 * q + 4, :].rearrange("e q n -> q e n"),
+            )
+        load_w2(0, 4)
+        load_w1(6)
+        load_w1(8)
+        load_w2(4, E)
+        load_w1(10)
+        gate_t = []
+        for h in range(2):
+            g = keep.tile([P, TOP, T], F32, name=f"gate_t{h}")
+            nc.sync.dma_start(out=g[:], in_=gate[:, P * h : P * (h + 1), :].rearrange("r p t -> p r t"))
+            gate_t.append(g)
+        pos_t = []
+        for r, pos in enumerate((pos1, pos2, pos3, pos4)):
+            pt = keep.tile([P, T // 16], U16, name=f"pos_t{r}")
+            nc.sync.dma_start(pt[:], pos)
+            pos_t.append(pt)
         x_bytes = []
         for s in range(PASSES):
             b = keep.tile([P, WINDOW], U8, name=f"x_bytes{s}", align_bytes=64)
             nc.vector.memset(b[:].bitcast(I32), 0)
             x_bytes.append(b)
-        pos_t = []
-        gate_t = {}
-
-        def load_w2_scales():
-            for q in range(4):
-                nc.sync.dma_start(
-                    out=w2s[32 * q : 32 * q + 4].bitcast(I32),
-                    in_=w2_scales32[:, 0, 4 * q : 4 * q + 4, :].rearrange("e q n -> q e n"),
-                )
-
-        def load_lists():
-            for r, pos in enumerate((pos1, pos2, pos3, pos4)):
-                pt = keep.tile([P, T // 16], U16, name=f"pos_t{r}")
-                nc.sync.dma_start(pt[:], pos)
-                pos_t.append(pt)
-
-        def load_gate(h):
-            gate_t[h] = w1_pool.tile([P, TOP, T], F32, name="w1w", align_bytes=64)
-            nc.sync.dma_start(out=gate_t[h][:], in_=gate[:, P * h : P * (h + 1), :].rearrange("r p t -> p r t"))
 
         x_words = []
         for s in range(PASSES):
@@ -131,17 +126,15 @@ def tile_moe_tk_mlp_relu_kernel(
             nc.vector.memset(w[:, T:], 0)
             x_words.append(w)
 
-        def quantise_tokens(s):
-            cut = SPLIT[s]
-            xa = keep.tile([P, cut, 4], BF16, name=f"xa{s}", align_bytes=64)
-            xb = keep.tile([P, T - cut, 4], BF16, name=f"xb{s}", align_bytes=64)
-            nc.vector.tensor_copy(out=xa[:], in_=raw[s][:, :, :cut].rearrange("p j w -> p w j"))
-            nc.scalar.copy(out=xb[:], in_=raw[s][:, :, cut:].rearrange("p j w -> p w j"))
-            for x, cols in ((xa, slice(0, cut)), (xb, slice(cut, T))):
+        def quantise_tokens(s, cut):
+            xb = keep.tile([P, T, 4], BF16, name=f"xb{s}", align_bytes=64)
+            nc.vector.tensor_copy(out=xb[:, :cut, :], in_=raw[s][:, :, :cut].rearrange("p j w -> p w j"))
+            nc.scalar.copy(out=xb[:, cut:, :], in_=raw[s][:, :, cut:].rearrange("p j w -> p w j"))
+            for cols in (slice(0, 256), slice(256, T)):
                 nc.vector.quantize_mx(
                     out=x_words[s][:, cols].bitcast(FP8X4),
                     scales=x_bytes[s][:, cols],
-                    in_=x[:].rearrange("p w j -> p (w j)"),
+                    in_=xb[:, cols, :].rearrange("p w j -> p (w j)"),
                 )
 
         y_t = []
@@ -236,27 +229,17 @@ def tile_moe_tk_mlp_relu_kernel(
 
         on_scalar = nc.scalar.copy
         on_vector = nc.vector.tensor_copy
-        quantise_tokens(0)
+        quantise_tokens(0, 256)
         gather_bytes(0, 0, 2)
         gather_words(0, 0, 2)
-        quantise_tokens(1)
+        quantise_tokens(1, 128)
         gather_bytes(1, 0, 2)
         gather_words(1, 0, 2)
-        load_w1_scales(nc.scalar, other_scales, 4, E)
-        load_w2(0, E)
-        plan = [
-            (-1.4, load_w2_scales, ()),
-            (-3.45, load_w1, (6,)),
-            (1.15, load_w1, (8,)),
-            (3.15, load_w1, (10,)),
-            (5.15, load_gate, (0,)),
-            (7.15, load_gate, (1,)),
-            (7.2, load_lists, ()),
-        ]
+        plan = []
         for e in range(2, E, 2):
             for s in range(PASSES):
-                plan.append((e - 2 + 0.03 * s, gather_bytes, (s, e, e + 2)))
-                plan.append((e - 2 + 0.03 * s + 0.01, gather_words, (s, e, e + 2)))
+                plan.append((e - 2 + 0.02 * s, gather_bytes, (s, e, e + 2)))
+                plan.append((e - 2 + 0.03 * s, gather_words, (s, e, e + 2)))
         for e in range(E):
             plan.append((e - 1.5, first_product, (e, 0)))
             plan.append((e + 0.1, first_product, (e, 1)))

from contextlib import ExitStack

import concourse.mybir as mybir
from concourse.masks import make_identity

F32 = mybir.dt.float32
BF16 = mybir.dt.bfloat16
I32 = mybir.dt.int32
U32 = mybir.dt.uint32
U16 = mybir.dt.uint16
U8 = mybir.dt.uint8
FP8X4 = mybir.dt.float8_e4m3fn_x4
FP4X4 = mybir.dt.float4_e2m1fn_x4
MULT = mybir.AluOpType.mult
RELU = mybir.ActivationFunctionType.Relu

K, T, E, C, H, N, TOP = 1024, 384, 12, 128, 512, 256, 4
P = 128
PASSES = K // 512
WINDOW = 512
FLOPS = 2 * TOP * T * (K * H + H * N)


def tile_moe_tk_mlp_relu_kernel(
    tc, xT, w1_words, w1_scales, w2_words, w2_scales, gate, offs, pos1, pos2, pos3, pos4, out
):
    nc = tc.nc
    with ExitStack() as ctx:
        keep = ctx.enter_context(tc.tile_pool(name="keep", bufs=1))
        words_pool = []
        for s in range(PASSES):
            words_pool.append(ctx.enter_context(tc.tile_pool(name=f"words_pool{s}", bufs=(2, 2)[s])))
        bytes_pool = []
        for s in range(PASSES):
            bytes_pool.append(ctx.enter_context(tc.tile_pool(name=f"bytes_pool{s}", bufs=2)))
        psum_a = ctx.enter_context(tc.psum_pool(name="psum_a", bufs=4))
        psum_t = ctx.enter_context(tc.psum_pool(name="psum_t", bufs=2))
        psum_y = ctx.enter_context(tc.psum_pool(name="psum_y", bufs=2))

        w1_words32 = w1_words.bitcast(I32)
        w1_scales32 = w1_scales.bitcast(I32)
        w2_words32 = w2_words.bitcast(I32)
        w2_scales32 = w2_scales.bitcast(I32)
        raw = []
        w1_at = {}
        w1s_at = {}
        w2_at = {}

        def load_x(s):
            r = keep.tile([P, 4, T], F32, name=f"raw{s}")
            nc.sync.dma_start(out=r[:], in_=xT[512 * s : 512 * (s + 1), :].rearrange("(p j) w -> p j w", j=4))
            raw.append(r)

        def load_w1(a):
            w = keep.tile([P, 2, PASSES, 2 * H], U8, name=f"w1w{a}", align_bytes=64)
            nc.sync.dma_start(
                out=w[:].rearrange("p e s w -> p (e s) w").bitcast(I32),
                in_=w1_words32[a : a + 2].rearrange("e s p w -> p (e s) w"),
            )
            for e in range(2):
                w1_at[a + e] = w[:, e]

        def load_w1_scales(a, b, zero):
            sc = keep.tile([P, b - a, PASSES, H], U8, name=f"w1s{a}", align_bytes=64)
            zero.memset(sc[:].rearrange("p e s i -> p (e s i)").bitcast(I32), 0)
            for q in range(4):
                nc.sync.dma_start(
                    out=sc[32 * q : 32 * q + 4].rearrange("p e s i -> p (e s) i").bitcast(I32),
                    in_=w1_scales32[a:b, :, 4 * q : 4 * q + 4, :].rearrange("e s q i -> q (e s) i"),
                )
            for e in range(a, b):
                w1s_at[e] = sc[:, e - a]

        def load_w2(a, b):
            w = keep.tile([P, b - a, 2 * N], U8, name=f"w2w{a}", align_bytes=64)
            nc.sync.dma_start(out=w[:].bitcast(I32), in_=w2_words32[a:b, 0].rearrange("e p w -> p e w"))
            for e in range(a, b):
                w2_at[e] = w[:, e - a]

        warm = keep.tile([P, 1], F32, name="warm")
        nc.gpsimd.memset(warm[:], 0.0)
        warm_out = keep.tile([P, 1], F32, name="warm_out")
        nc.scalar.activation(warm_out[:], warm[:], RELU)
        ident = keep.tile([P, P], F32, name="ident")
        make_identity(nc, ident[:])
        load_x(0)
        load_x(1)
        offs_t = keep.tile([P, TOP * T // 16], U16, name="offs_t")
        nc.sync.dma_start(offs_t[:], offs)
        load_w1(0)
        load_w1_scales(0, 4, nc.vector)
        load_w1(2)
        load_w1(4)
        load_w1_scales(4, E, nc.gpsimd)
        w2s = keep.tile([P, E, N], U8, name="w2s", align_bytes=64)
        nc.gpsimd.memset(w2s[:].rearrange("p e n -> p (e n)").bitcast(I32), 0)
        for q in range(4):
            nc.sync.dma_start(
                out=w2s[32 * q : 32 * q + 4].bitcast(I32),
                in_=w2_scales32[:, 0, 4 * q : 4 * q + 4, :].rearrange("e q n -> q e n"),
            )
        load_w2(0, 4)
        load_w1(6)
        load_w1(8)
        load_w2(4, E)
        load_w1(10)
        gate_t = []
        for h in range(2):
            g = keep.tile([P, TOP, T], F32, name=f"gate_t{h}")
            nc.sync.dma_start(out=g[:], in_=gate[:, P * h : P * (h + 1), :].rearrange("r p t -> p r t"))
            gate_t.append(g)
        pos_t = []
        for r, pos in enumerate((pos1, pos2, pos3, pos4)):
            pt = keep.tile([P, T // 16], U16, name=f"pos_t{r}")
            nc.sync.dma_start(pt[:], pos)
            pos_t.append(pt)
        x_bytes = []
        for s in range(PASSES):
            b = keep.tile([P, WINDOW], U8, name=f"x_bytes{s}", align_bytes=64)
            nc.vector.memset(b[:].bitcast(I32), 0)
            x_bytes.append(b)

        x_words = []
        for s in range(PASSES):
            w = keep.tile([P, WINDOW], I32, name=f"x_words{s}", align_bytes=64)
            nc.vector.memset(w[:, T:], 0)
            x_words.append(w)

        def quantise_tokens(s, cut):
            xb = keep.tile([P, T, 4], BF16, name=f"xb{s}", align_bytes=64)
            nc.vector.tensor_copy(out=xb[:, :cut, :], in_=raw[s][:, :, :cut].rearrange("p j w -> p w j"))
            nc.scalar.copy(out=xb[:, cut:, :], in_=raw[s][:, :, cut:].rearrange("p j w -> p w j"))
            for cols in (slice(0, 256), slice(256, T)):
                nc.vector.quantize_mx(
                    out=x_words[s][:, cols].bitcast(FP8X4),
                    scales=x_bytes[s][:, cols],
                    in_=xb[:, cols, :].rearrange("p w j -> p (w j)"),
                )

        y_t = []
        for h in range(2):
            y = keep.tile([P, TOP * T], F32, name=f"y_t{h}")
            y_t.append(y)

        bytes_at = {}
        words_at = {}
        acc_at = {}
        act_at = {}
        turned_at = {}
        ready_at = {}
        hidden_at = {}
        yp_at = {}

        def gather_bytes(s, a, b):
            gb = bytes_pool[s].tile([P, C * (b - a)], U8, name=f"bytes{s}", align_bytes=64)
            nc.vector.tensor_copy(gb[:], x_bytes[s][:].indirect(offs_t[:, C // 16 * a : C // 16 * b]))
            for e in range(a, b):
                bytes_at[e, s] = gb[:, C * (e - a) : C * (e - a + 1)]

        def gather_words(s, a, b):
            gw = words_pool[s].tile([P, C * (b - a)], U32, name=f"words{s}", align_bytes=64)
            nc.vector.tensor_copy(gw[:], x_words[s][:].bitcast(U32).indirect(offs_t[:, C // 16 * a : C // 16 * b]))
            for e in range(a, b):
                words_at[e, s] = gw[:, C * (e - a) : C * (e - a + 1)]

        def first_product(e, s):
            if s == 0:
                acc_at[e] = psum_a.tile([P, H], F32, name="acc")
            nc.tensor.matmul_mx(
                out=acc_at[e][:],
                lhsT=words_at[e, s].bitcast(FP8X4),
                lhsT_scale=bytes_at[e, s],
                rhs=w1_at[e][:, s, :].bitcast(FP4X4),
                rhs_scale=w1s_at[e][:, s, :],
                start=(s == 0),
                stop=(s == PASSES - 1),
            )

        def relu(e):
            act = keep.tile([P, H], BF16, name=f"act{e}")
            nc.scalar.activation(
                act[:].rearrange("p (u m d) -> p u m d", u=2, d=2),
                acc_at[e][:].rearrange("p (m u d) -> p u m d", u=2, d=2),
                RELU,
            )
            act_at[e] = act

        def turn(e, a, b):
            if e == a:
                turned_at[a] = psum_t.tile([P, 2, 2, C], F32, name="tp")
            for u in range(2):
                nc.tensor.transpose(
                    turned_at[a][:, e - a, u, :], act_at[e][:].bitcast(F32)[:, C * u : C * (u + 1)], ident[:]
                )

        def interleave(copy, a, b):
            ht = keep.tile([P, (b - a) * C * 4], BF16, name=f"ht{a}", align_bytes=64)
            copy(
                out=ht[:].bitcast(F32).rearrange("p (i r u) -> p i r u", i=b - a, u=2),
                in_=turned_at[a][:, : b - a].rearrange("p i u r -> p i r u"),
            )
            ready_at[a] = ht

        def quantise_hidden(a, b):
            hw = keep.tile([P, (b - a) * C], U32, name=f"hw{a}", align_bytes=64)
            hb = keep.tile([P, (b - a) * C], U8, name=f"hb{a}", align_bytes=64)
            nc.vector.quantize_mx(out=hw[:].bitcast(FP8X4), scales=hb[:], in_=ready_at[a][:])
            for e in range(a, b):
                cols = slice(C * (e - a), C * (e - a + 1))
                hidden_at[e] = (hw[:, cols], hb[:, cols])

        def second_product(e):
            if e % 2 == 0:
                yp_at[e // 2] = psum_y.tile([P, 2, 2 * C], F32, name="yp")
            hw, hb = hidden_at[e]
            for h in range(2):
                nc.tensor.matmul_mx(
                    out=yp_at[e // 2][:, h, C * (e % 2) : C * (e % 2 + 1)],
                    lhsT=w2_at[e][:, 2 * P * h : 2 * P * (h + 1)].bitcast(FP4X4),
                    lhsT_scale=w2s[:, e, P * h : P * (h + 1)],
                    rhs=hw.bitcast(FP8X4),
                    rhs_scale=hb,
                    start=True,
                    stop=True,
                )

        def keep_y(copy, e, h):
            copy(out=y_t[h][:, C * e : C * (e + 2)], in_=yp_at[e // 2][:, h, :])

        on_scalar = nc.scalar.copy
        on_vector = nc.vector.tensor_copy
        quantise_tokens(0, 256)
        gather_bytes(0, 0, 2)
        gather_words(0, 0, 2)
        quantise_tokens(1, 128)
        gather_bytes(1, 0, 2)
        gather_words(1, 0, 2)
        plan = []
        for e in range(2, E, 2):
            for s in range(PASSES):
                plan.append((e - 2 + 0.02 * s, gather_bytes, (s, e, e + 2)))
                plan.append((e - 2 + 0.03 * s, gather_words, (s, e, e + 2)))
        for e in range(E):
            plan.append((e - 1.5, first_product, (e, 0)))
            plan.append((e + 0.1, first_product, (e, 1)))
            plan.append((e + 0.2, relu, (e,)))
        for a, b in ((0, 2), (2, 4), (4, 6), (6, 8), (8, 10), (10, 11), (11, 12)):
            for e in range(a, b):
                plan.append((b - 1 + 2 + 0.3, turn, (e, a, b)))
                plan.append((b - 1 + 3 + 1.5 + 0.6, second_product, (e,)))
            plan.append((b - 1 + 2.5 + 0.4, interleave, (on_vector if 99 <= a < 99 else on_scalar, a, b)))
            plan.append((b - 1 + 3 + 0.5, quantise_hidden, (a, b)))
        for e in range(0, E, 2):
            for h in range(2):
                plan.append((e + 1 + 3 + 2 + 0.7, keep_y, (on_vector if h == 1 and e >= 99 else on_scalar, e, h)))
        for when, step, what in sorted(plan, key=lambda entry: entry[0]):
            step(*what)

        z = []
        part = []
        o = []
        for h in range(2):
            zt = keep.tile([P, TOP, T], F32, name=f"z{h}")
            pt = keep.tile([P, 2, T], F32, name=f"part{h}")
            ot = keep.tile([P, T], F32, name=f"o{h}")
            z.append(zt)
            part.append(pt)
            o.append(ot)

        def fetch(h, r):
            nc.vector.tensor_tensor(z[h][:, r, :], y_t[h][:].indirect(pos_t[r][:]), gate_t[h][:, r, :], MULT)

        def store(h):
            nc.sync.dma_start(out=out[P * h : P * (h + 1), :], in_=o[h][:])

        for r in range(TOP):
            fetch(0, r)
        fetch(1, 0)
        fetch(1, 1)
        nc.vector.tensor_add(part[0][:], z[0][:, 0:2, :], z[0][:, 2:4, :])
        fetch(1, 2)
        nc.vector.tensor_add(part[1][:, 0, :], z[1][:, 0, :], z[1][:, 1, :])
        nc.vector.tensor_add(o[0][:], part[0][:, 0, :], part[0][:, 1, :])
        store(0)
        nc.vector.tensor_add(part[1][:, 1, :], part[1][:, 0, :], z[1][:, 2, :])
        fetch(1, 3)
        nc.vector.tensor_add(o[1][:], part[1][:, 1, :], z[1][:, 3, :])
        store(1)
